import numpy as np
import ml_dtypes


def mxq(x, axis, fmt="e4m3"):
    dtype, down = {"e4m3": (ml_dtypes.float8_e4m3fn, 7), "e5m2": (ml_dtypes.float8_e5m2, 14)}[fmt]
    v = np.moveaxis(np.asarray(x, np.float32).astype(ml_dtypes.bfloat16).astype(np.float64), axis, -1)
    blocks = v.reshape(v.shape[:-1] + (-1, 32))
    amax = np.abs(blocks).max(-1, keepdims=True)
    byte = np.maximum(np.where(amax > 0, np.frexp(amax)[1] - 1 + 127, 0) - down, 1)
    scale = np.exp2(byte - 127.0)
    codes = (blocks / scale).astype(np.float32).astype(dtype).astype(np.float64)
    return np.moveaxis((codes * scale).reshape(v.shape), -1, axis)


WIDE = False


def mx_kscale(k):
    if not WIDE:
        return np.ones(k)
    levels = np.array([10, -10, 5, -5, 0])
    if k % 512:
        return np.exp2(np.random.permutation(np.resize(levels, k // 32))).repeat(32)
    a = np.empty((k // 512, 16))
    for p in range(k // 512):
        a[p, :8] = np.random.permutation(np.resize(levels, 8))
        for g in range(8):
            far = levels[np.abs(levels - a[p, g]) >= 10]
            a[p, g + 8] = far[np.random.randint(len(far))]
    return np.exp2(a.ravel()).repeat(32)


BF16 = ml_dtypes.bfloat16


def bf(x):
    return np.asarray(x, np.float32).astype(BF16)


def f64(x):
    return np.asarray(x).astype(np.float64)


E2M1 = np.array([0.0, 0.5, 1.0, 1.5, 2.0, 3.0, 4.0, 6.0, -0.0, -0.5, -1.0, -1.5, -2.0, -3.0, -4.0, -6.0])


def pack_weight(w, fmt):
    k, n = w.shape
    w = f64(bf(w)).reshape(k // 32, 32, n)
    amax = np.abs(w).max(1)
    if fmt == "e4m3":
        byte = np.frexp(amax)[1] - 1 + 127 - 7
    else:
        mant, ex = np.frexp(amax / 6.0)
        byte = np.where(mant > 0.5, ex, ex - 1) + 127
    byte = np.clip(np.where(amax > 0, byte, 1), 1, 254)
    scaled = (w * np.exp2(127.0 - byte)[:, None, :]).reshape(k, n).astype(np.float32)
    by_word = np.ascontiguousarray(scaled.reshape(k // 512, 128, 4, n).transpose(0, 1, 3, 2))
    if fmt == "e4m3":
        words = by_word.astype(ml_dtypes.float8_e4m3fn).view(np.uint8)
    else:
        c = by_word.astype(ml_dtypes.float4_e2m1fn).view(np.uint8) & 0xF
        words = c[..., 0::2] | (c[..., 1::2] << 4)
    return np.ascontiguousarray(words), np.ascontiguousarray(byte.astype(np.uint8).reshape(k // 512, 16, n))


def unpack_weight(words, scales, fmt):
    g, p, n, _ = words.shape
    if fmt == "e4m3":
        vals = np.ascontiguousarray(words).view(ml_dtypes.float8_e4m3fn).astype(np.float64)
    else:
        nib = np.empty((g, p, n, 4), np.uint8)
        nib[..., 0::2] = words & 0xF
        nib[..., 1::2] = words >> 4
        vals = E2M1[nib]
    vals = vals * np.repeat(np.exp2(scales.astype(np.float64) - 127.0), 8, axis=1)[..., None]
    return vals.transpose(0, 1, 3, 2).reshape(g * 512, n)
def pack4(w):
    words, scales = pack_weight(w, "e2m1")
    return words.reshape(words.shape[0], 128, -1), scales


def unpack4(words, scales):
    return unpack_weight(words.reshape(words.shape[0], 128, -1, 2), scales, "e2m1")


T, V, F, D = 1024, 1536, 2048, 1024


def setup_inputs():
    s = mx_kscale(V)
    c = mx_kscale(F)
    u = mx_kscale(T)
    y = np.random.standard_normal((F, T)) * c[:, None] / u
    b = np.random.standard_normal((F, D)) / np.sqrt(F) / c[:, None]
    y_words, y_scales = pack4(y)
    b_words, b_scales = pack4(b)
    return {"x": bf(np.random.standard_normal((T, V)) * s),
            "rot": bf(np.random.standard_normal((V, D)) / np.sqrt(V) / s[:, None]),
            "weight": bf((0.5 + np.random.random(T)) * u),
            "y_words": y_words, "y_scales": y_scales,
            "b_words": b_words, "b_scales": b_scales,
            "gain": bf((1 + 0.1 * np.random.standard_normal(D)) / np.sqrt(T)),
            "prior": bf(0.5 * np.random.standard_normal((D, D)))}


def reference(x, rot, weight, y_words, y_scales, b_words, b_scales, gain, prior):
    aligned = mxq(f64(x), 1, "e4m3") @ mxq(f64(rot), 0, "e4m3")
    aligned = aligned * f64(weight)[:, None]
    template = unpack4(y_words, y_scales).T @ unpack4(b_words, b_scales)
    cross = mxq(aligned, 0, "e4m3").T @ mxq(template, 0, "e4m3")
    return cross * f64(gain) + f64(prior)

@@ -1,0 +1,396 @@
+from contextlib import ExitStack
+
+import concourse.mybir as mybir
+from concourse.masks import make_identity
+
+F32 = mybir.dt.float32
+BF16 = mybir.dt.bfloat16
+I32 = mybir.dt.int32
+U32 = mybir.dt.uint32
+U8 = mybir.dt.uint8
+FP8X4 = mybir.dt.float8_e4m3fn_x4
+FP4X4 = mybir.dt.float4_e2m1fn_x4
+MULT = mybir.AluOpType.mult
+ADD = mybir.AluOpType.add
+
+T, V, F, D = 1024, 1536, 2048, 1024
+P = 128
+GX = V // 512
+GY = F // 512
+FLOPS = 2 * T * D * (V + F) + 2 * D * D * T
+
+
+def tile_hyperalignment_cross_product_s12_kernel(
+    tc, x, rot, weight, y_words, y_scales, b_words, b_scales, gain, prior, out
+):
+    nc = tc.nc
+    with ExitStack() as ctx:
+        keep = ctx.enter_context(tc.tile_pool(name="keep", bufs=1))
+        stage = ctx.enter_context(tc.tile_pool(name="stage", bufs=4))
+        pair = ctx.enter_context(tc.tile_pool(name="pair", bufs=2))
+        work = ctx.enter_context(tc.tile_pool(name="work", bufs=5))
+        psum = ctx.enter_context(tc.psum_pool(name="psum", bufs=4))
+        ctx.enter_context(tc.manual_schedule())
+
+        def kt(name, shape, dtype):
+            return keep.tile(shape, dtype, name=name, tag=name, align_bytes=64)
+
+        x_sb = [kt(f"x{m}", [P, V], BF16) for m in range(8)]
+        ysr = kt("ysr", [P, GY * T], U8)
+        ysp = kt("ysp", [P, GY * T], U8)
+        bs = kt("bs", [P, GY, D], U8)
+        yraw = [kt(f"yraw{h}", [P, GY * 1024], U8) for h in range(2)]
+        yp = [kt(f"yp{h}", [P, GY * 1024], U8) for h in range(2)]
+        braw = [kt(f"braw{e}", [P, GY, 1024], U8) for e in range(2)]
+        rraw = [[kt(f"rraw{e}{g}", [P, 4, 512], BF16) for g in range(GX)] for e in range(2)]
+        rc = [[kt(f"rc{e}{g}", [P, 512], U32) for g in range(GX)] for e in range(2)]
+        rs = [[kt(f"rs{e}{g}", [P, 512], U8) for g in range(GX)] for e in range(2)]
+        xin = [[kt(f"xin{h}{g}", [P, 2048], BF16) for g in range(GX)] for h in range(2)]
+        xc = [[kt(f"xc{h}{g}", [P, 512], U32) for g in range(GX)] for h in range(2)]
+        xs = [[kt(f"xs{h}{g}", [P, 512], U8) for g in range(GX)] for h in range(2)]
+        tin = [kt(f"tin{h}", [P, 512, 4], BF16) for h in range(2)]
+        tcd = [kt(f"tcd{h}", [P, 512], U32) for h in range(2)]
+        tsc = [kt(f"tsc{h}", [P, 512], U8) for h in range(2)]
+        ucd = [kt(f"ucd{n}", [P, 2, 128], U32) for n in range(4)]
+        usc = [kt(f"usc{n}", [P, 2, 128], U8) for n in range(4)]
+        acd = [kt(f"acd{c}", [P, 2, 128], U32) for c in range(8)]
+        asc = [kt(f"asc{c}", [P, 2, 128], U8) for c in range(8)]
+        pr = kt("pr", [P, 8, D], BF16)
+        gb = kt("gb", [P, D], BF16)
+        ident = kt("ident", [P, P], F32)
+        perm = kt("perm", [P, P], F32)
+        identb = kt("identb", [P, P], BF16)
+        wrow = kt("wrow", [P, P], BF16)
+        wcol = kt("wcol", [P, 8], BF16)
+        wcolf = kt("wcolf", [P, 8], F32)
+
+        def load_x(m):
+            nc.sync.dma_start(out=x_sb[m][:], in_=x[128 * m : 128 * m + 128, :])
+
+        def load_scales(plane, dram):
+            for q in range(4):
+                nc.sync.dma_start(
+                    out=plane[32 * q : 32 * q + 4, :].bitcast(I32).rearrange("r (g n) -> r g n", g=GY),
+                    in_=dram[:, 4 * q : 4 * q + 4, :].bitcast(I32).rearrange("g r n -> r g n"),
+                )
+
+        def load_words(tile, dram, half):
+            nc.sync.dma_start(
+                out=tile.bitcast(I32).rearrange("p (g n) -> p g n", g=GY),
+                in_=dram[:, :, 1024 * half : 1024 * half + 1024].bitcast(I32).rearrange("g p n -> p g n"),
+            )
+
+        nc.vector.memset(ysr[:].bitcast(I32), 0)
+        nc.vector.memset(bs[:].rearrange("p g n -> p (g n)").bitcast(I32), 0)
+        make_identity(nc, ident[:])
+        nc.gpsimd.memset(wrow[:], 0.0)
+        nc.vector.tensor_copy(
+            out=perm[:].rearrange("p (j a i) -> p j a i", j=4, a=4),
+            in_=ident[:].rearrange("p (a j i) -> p j a i", a=4, j=4),
+        )
+        nc.vector.tensor_copy(out=identb[:], in_=ident[:])
+
+        rot_v = rot.rearrange("(g p j) d -> g p j d", g=GX, j=4)
+        pr_v = prior.rearrange("(c p) e -> p c e", p=128)
+
+        def load_rot(e):
+            for g in range(GX):
+                nc.sync.dma_start(out=rraw[e][g][:], in_=rot_v[g][:, :, 512 * e : 512 * e + 512])
+
+        load_x(0)
+        load_scales(ysr[:], y_scales)
+        for m in range(1, 5):
+            load_x(m)
+        load_scales(bs[:].rearrange("p g n -> p (g n)"), b_scales)
+        load_x(5)
+        load_words(yraw[0][:], y_words, 0)
+        load_words(braw[0][:].rearrange("p g n -> p (g n)"), b_words, 0)
+        load_x(6)
+        load_x(7)
+        load_words(yraw[1][:], y_words, 1)
+        for h in range(2):
+            nc.sync.dma_start(
+                out=wrow[4 * h : 4 * h + 4, :].rearrange("j (q i) -> j q i", i=8),
+                in_=weight.rearrange("(h q j i) -> h j q i", h=2, j=4, i=8)[h],
+            )
+        load_rot(0)
+        nc.sync.dma_start(out=gb[:], in_=gain.partition_broadcast(128))
+        load_rot(1)
+        nc.sync.dma_start(out=pr[:, 0:4, :], in_=pr_v[:, 0:4, :])
+        load_words(braw[1][:].rearrange("p g n -> p (g n)"), b_words, 1)
+        nc.sync.dma_start(out=pr[:, 4:8, :], in_=pr_v[:, 4:8, :])
+
+        rin = {}
+
+        def xpose(tiles, engines):
+            todo = [(m, g) for m in tiles for g in range(GX)]
+            for k in range(0, len(todo), 2):
+                two = todo[k : k + 2]
+                on_scalar = engines[(k // 2) % len(engines)] == "S"
+                bank = psum.tile([P, 2, 2, 128], F32, name="bank", tag="tr")
+                for s, (m, g) in enumerate(two):
+                    words = x_sb[m][:].bitcast(F32)
+                    for u in range(2):
+                        nc.tensor.transpose(
+                            bank[:, s, u, :], words[:, 256 * g + u : 256 * (g + 1) : 2], perm[:]
+                        )
+                for s, (m, g) in enumerate(two):
+                    h, mm = m // 4, m % 4
+                    dst = xin[h][g][:].bitcast(F32).rearrange("p (j c u) -> p j c u", j=4, u=2)
+                    dst = dst[:, :, 32 * mm : 32 * mm + 32, :]
+                    srcv = bank[:, s, :, :].rearrange("p u (j c) -> p j c u", j=4)
+                    if on_scalar:
+                        nc.scalar.copy(out=dst, in_=srcv)
+                    else:
+                        nc.vector.tensor_copy(out=dst, in_=srcv)
+
+        def permute_y(h):
+            nc.vector.tensor_copy(
+                out=yp[h][:].bitcast(I32).rearrange("p (j s w) -> p j s w", j=4, w=4),
+                in_=yraw[h][:].bitcast(I32).rearrange("p (s j w) -> p j s w", j=4, w=4),
+            )
+
+        def permute_ys():
+            nc.vector.tensor_copy(
+                out=ysp[:].bitcast(I32).rearrange("p (j s w) -> p j s w", j=4, w=2),
+                in_=ysr[:].bitcast(I32).rearrange("p (s j w) -> p j s w", j=4, w=2),
+            )
+
+        def template(h, e, n, dst):
+            bank = psum.tile([P, 4, 128], F32, name="ev", tag="ev")
+            for j in range(4):
+                for g in range(GY):
+                    nc.tensor.matmul_mx(
+                        out=bank[:, j, :],
+                        lhsT=yp[h][:, 1024 * j + 256 * g : 1024 * j + 256 * g + 256].bitcast(FP4X4),
+                        lhsT_scale=ysp[:, 1024 * j + 256 * g + 128 * h : 1024 * j + 256 * g + 128 * h + 128],
+                        rhs=braw[e][:, g, 256 * n : 256 * n + 256].bitcast(FP4X4),
+                        rhs_scale=bs[:, g, 512 * e + 128 * n : 512 * e + 128 * n + 128],
+                        start=(g == 0),
+                        stop=(g == GY - 1),
+                    )
+            nc.scalar.copy(out=dst, in_=bank[:].rearrange("p j n -> p n j"))
+
+        def template_wide(h, n2):
+            for jp in range(2):
+                bank = psum.tile([P, 2, 256], F32, name="ev", tag="ev")
+                for k in range(2):
+                    j = 2 * jp + k
+                    for g in range(GY):
+                        nc.tensor.matmul_mx(
+                            out=bank[:, k, :],
+                            lhsT=yp[h][:, 1024 * j + 256 * g : 1024 * j + 256 * g + 256].bitcast(FP4X4),
+                            lhsT_scale=ysp[:, 1024 * j + 256 * g + 128 * h : 1024 * j + 256 * g + 128 * h + 128],
+                            rhs=braw[0][:, g, 512 * n2 : 512 * n2 + 512].bitcast(FP4X4),
+                            rhs_scale=bs[:, g, 256 * n2 : 256 * n2 + 256],
+                            start=(g == 0),
+                            stop=(g == GY - 1),
+                        )
+                nc.scalar.copy(
+                    out=tin[h][:, 256 * n2 : 256 * n2 + 256, 2 * jp : 2 * jp + 2],
+                    in_=bank[:].rearrange("p j n -> p n j"),
+                )
+
+        def quant(codes, scales, src):
+            nc.vector.quantize_mx(out=codes.bitcast(FP8X4), scales=scales, in_=src)
+
+        def quant_x(h, g):
+            quant(xc[h][g][:], xs[h][g][:], xin[h][g][:])
+
+        def inter_rot(e, g, on_scalar):
+            rin[e, g] = stage.tile([P, 2048], BF16, name="rin", tag="rin", align_bytes=64)
+            dst = rin[e, g][:].rearrange("p (c i t) -> p c t i", i=4, t=4)
+            srcv = rraw[e][g][:].rearrange("p t (c i) -> p c t i", i=4)
+            if on_scalar:
+                nc.scalar.copy(out=dst, in_=srcv)
+            else:
+                nc.vector.tensor_copy(out=dst, in_=srcv)
+
+        def quant_rot(e, g):
+            quant(rc[e][g][:], rs[e][g][:], rin[e, g][:])
+
+        def aligned_mm(c):
+            e, cc = c // 4, c % 4
+            banks = []
+            for h in range(2):
+                bank = psum.tile([P, 4, 128], F32, name="ev", tag="ev")
+                for j in range(4):
+                    for g in range(GX):
+                        nc.tensor.matmul_mx(
+                            out=bank[:, j, :],
+                            lhsT=xc[h][g][:, 128 * j : 128 * j + 128].bitcast(FP8X4),
+                            lhsT_scale=xs[h][g][:, 128 * j : 128 * j + 128],
+                            rhs=rc[e][g][:, 128 * cc : 128 * cc + 128].bitcast(FP8X4),
+                            rhs_scale=rs[e][g][:, 128 * cc : 128 * cc + 128],
+                            start=(g == 0),
+                            stop=(g == GX - 1),
+                        )
+                banks.append(bank)
+            return banks
+
+        def aligned_weigh(banks, share):
+            ain = pair.tile([P, 2, 128, 4], BF16, name="ain", tag="ain", align_bytes=64)
+            for h in range(2):
+                if h == 0 and share:
+                    for j in range(4):
+                        nc.scalar.activation(
+                            out=ain[:, h, :, j],
+                            in_=banks[h][:, j, :],
+                            func=mybir.ActivationFunctionType.Copy,
+                            scale=wcolf[:, 4 * h + j : 4 * h + j + 1],
+                        )
+                    continue
+                nc.vector.tensor_tensor(
+                    out=ain[:, h, :, :],
+                    in0=banks[h][:].rearrange("p j n -> p n j"),
+                    in1=wcol[:, 4 * h : 4 * h + 4].unsqueeze(1).to_broadcast([P, 128, 4]),
+                    op=MULT,
+                )
+            return ain
+
+        def aligned_quant(c, ain):
+            quant(
+                acd[c][:].rearrange("p h n -> p (h n)"),
+                asc[c][:].rearrange("p h n -> p (h n)"),
+                ain[:].rearrange("p h n j -> p (h n j)"),
+            )
+
+        def cross_wide(c):
+            bank = psum.tile([P, 512], F32, name="st", tag="tr")
+            for h in range(2):
+                nc.tensor.matmul_mx(
+                    out=bank[:],
+                    lhsT=acd[c][:, h, :].bitcast(FP8X4),
+                    lhsT_scale=asc[c][:, h, :],
+                    rhs=tcd[h][:].bitcast(FP8X4),
+                    rhs_scale=tsc[h][:],
+                    start=(h == 0),
+                    stop=(h == 1),
+                )
+            return bank
+
+        def gain_wide(bank):
+            tmp = work.tile([P, 512], F32, name="tmp", tag="tmp")
+            nc.vector.tensor_tensor(out=tmp[:], in0=bank[:], in1=gb[:, 0:512], op=MULT)
+            return tmp
+
+        def finish_wide(c, tmp, eng):
+            res = work.tile([P, 512], F32, name="res", tag="res")
+            eng.tensor_tensor(out=res[:], in0=tmp[:], in1=pr[:, c, 0:512], op=ADD)
+            nc.sync.dma_start(out=out[128 * c : 128 * c + 128, 0:512], in_=res[:])
+
+        def template_quant(n, src):
+            quant(
+                ucd[n][:].rearrange("p h n -> p (h n)"),
+                usc[n][:].rearrange("p h n -> p (h n)"),
+                src[:].rearrange("p h n j -> p (h n j)"),
+            )
+
+        def cross_narrow(n, c0, count):
+            bank = psum.tile([P, 4, 128], F32, name="st", tag="tr")
+            for k in range(count):
+                c = c0 + k
+                for h in range(2):
+                    nc.tensor.matmul_mx(
+                        out=bank[:, k, :],
+                        lhsT=acd[c][:, h, :].bitcast(FP8X4),
+                        lhsT_scale=asc[c][:, h, :],
+                        rhs=ucd[n][:, h, :].bitcast(FP8X4),
+                        rhs_scale=usc[n][:, h, :],
+                        start=(h == 0),
+                        stop=(h == 1),
+                    )
+            return bank
+
+        def gain_narrow(n, count, bank):
+            cols = slice(512 + 128 * n, 512 + 128 * n + 128)
+            tmp = work.tile([P, 4, 128], F32, name="tmp", tag="tmp")
+            nc.vector.tensor_tensor(
+                out=tmp[:, 0:count, :],
+                in0=bank[:, 0:count, :],
+                in1=gb[:, cols].unsqueeze(1).to_broadcast([P, count, 128]),
+                op=MULT,
+            )
+            return tmp
+
+        def finish_narrow(n, c0, count, tmp, eng):
+            cols = slice(512 + 128 * n, 512 + 128 * n + 128)
+            res = work.tile([P, 4, 128], F32, name="res", tag="res")
+            eng.tensor_tensor(
+                out=res[:, 0:count, :], in0=tmp[:, 0:count, :], in1=pr[:, c0 : c0 + count, cols], op=ADD
+            )
+            nc.sync.dma_start(
+                out=out.rearrange("(c p) e -> p c e", p=128)[:, c0 : c0 + count, cols], in_=res[:, 0:count, :]
+            )
+
+        xpose([0, 1, 2, 3], "SV")
+        xpose([4, 5], "SVS")
+        permute_ys()
+        quant_x(0, 0)
+        permute_y(0)
+        template_wide(0, 0)
+        quant_x(0, 1)
+        quant_x(0, 2)
+        xpose([6, 7], "SVS")
+        permute_y(1)
+        wbank = psum.tile([P, P], BF16, name="wbank", tag="tr")
+        nc.tensor.transpose(wbank[:], wrow[:], identb[:])
+        nc.vector.tensor_copy(out=wcol[:], in_=wbank[:, 0:8])
+        template_wide(0, 1)
+        quant_x(1, 0)
+        nc.vector.tensor_copy(out=wcolf[:], in_=wcol[:])
+        quant_x(1, 1)
+        quant_x(1, 2)
+        inter_rot(0, 0, False)
+        inter_rot(0, 2, True)
+        inter_rot(0, 1, False)
+        template_wide(1, 0)
+        quant_rot(0, 0)
+        quant_rot(0, 1)
+        quant_rot(0, 2)
+        quant(tcd[0][:], tsc[0][:], tin[0][:].rearrange("p n j -> p (n j)"))
+        template_wide(1, 1)
+
+        pending = None
+        tmp = None
+        for c in range(8):
+            banks = aligned_mm(c)
+            if pending is not None:
+                st = cross_wide(pending)
+            ain = aligned_weigh(banks, c in (4, 5, 6, 7))
+            if c == 0:
+                quant(tcd[1][:], tsc[1][:], tin[1][:].rearrange("p n j -> p (n j)"))
+            if c == 3:
+                quant_rot(1, 2)
+            if pending is not None:
+                tmp = gain_wide(st)
+            aligned_quant(c, ain)
+            if pending is not None:
+                finish_wide(pending, tmp, nc.gpsimd if c in (1, 2, 3, 4) else nc.vector)
+            pending = c
+            if c in (1, 2):
+                quant_rot(1, c - 1)
+            if c < 3:
+                inter_rot(1, c, True)
+
+        uin = {}
+        for n in range(4):
+            uin[n] = pair.tile([P, 2, 128, 4], BF16, name="uin", tag="uin", align_bytes=64)
+            for h in range(2):
+                template(h, 1, n, uin[n][:, h, :, :])
+            if n == 0:
+                st = cross_wide(7)
+                tmp = gain_wide(st)
+                template_quant(0, uin[0])
+                finish_wide(7, tmp, nc.vector)
+                continue
+            sts = [cross_narrow(n - 1, c0, 4) for c0 in (0, 4)]
+            template_quant(n, uin[n])
+            tmps = [gain_narrow(n - 1, 4, st) for st in sts]
+            for c0, tmp in zip((0, 4), tmps):
+                finish_narrow(n - 1, c0, 4, tmp, nc.gpsimd if n == 3 else nc.vector)
+        parts = [(0, 4), (4, 2), (6, 2)]
+        sts = [cross_narrow(3, c0, count) for c0, count in parts]
+        tmps = [gain_narrow(3, count, st) for (c0, count), st in zip(parts, sts)]
+        for (c0, count), tmp in zip(parts, tmps):
+            finish_narrow(3, c0, count, tmp, nc.gpsimd if c0 == 4 else nc.vector)

@@ -36,9 +36,9 @@ def tile_hyperalignment_cross_product_s12_kernel(
             return keep.tile(shape, dtype, name=name, tag=name, align_bytes=64)
 
         x_sb = [kt(f"x{m}", [P, V], BF16) for m in range(8)]
-        ysr = kt("ysr", [P, GY * T], U8)
-        ysp = kt("ysp", [P, GY * T], U8)
-        bs = kt("bs", [P, GY, D], U8)
+        ysr = [kt(f"ysr{h}", [P, GY * 512], U8) for h in range(2)]
+        ysp = [kt(f"ysp{h}", [P, GY * 512], U8) for h in range(2)]
+        bs = [kt(f"bs{e}", [P, GY, 512], U8) for e in range(2)]
         yraw = [kt(f"yraw{h}", [P, GY * 1024], U8) for h in range(2)]
         yp = [kt(f"yp{h}", [P, GY * 1024], U8) for h in range(2)]
         braw = [kt(f"braw{e}", [P, GY, 1024], U8) for e in range(2)]
@@ -51,27 +51,31 @@ def tile_hyperalignment_cross_product_s12_kernel(
         tin = [kt(f"tin{h}", [P, 512, 4], BF16) for h in range(2)]
         tcd = [kt(f"tcd{h}", [P, 512], U32) for h in range(2)]
         tsc = [kt(f"tsc{h}", [P, 512], U8) for h in range(2)]
-        ucd = [kt(f"ucd{n}", [P, 2, 128], U32) for n in range(4)]
-        usc = [kt(f"usc{n}", [P, 2, 128], U8) for n in range(4)]
+        uin, ucd, usc = {}, {}, {}
         acd = [kt(f"acd{c}", [P, 2, 128], U32) for c in range(8)]
         asc = [kt(f"asc{c}", [P, 2, 128], U8) for c in range(8)]
         pr = kt("pr", [P, 8, D], BF16)
         gb = kt("gb", [P, D], BF16)
         ident = kt("ident", [P, P], F32)
+        blank = kt("blank", [P, 2048], BF16)
+        blank_codes = kt("blank_codes", [P, 512], U32)
+        blank_scales = kt("blank_scales", [P, 512], U8)
         perm = kt("perm", [P, P], F32)
         identb = kt("identb", [P, P], BF16)
         wrow = kt("wrow", [P, P], BF16)
-        wcol = kt("wcol", [P, 8], BF16)
+        wcol = kt("wcol", [P, 16], BF16)
         wcolf = kt("wcolf", [P, 8], F32)
 
         def load_x(m):
             nc.sync.dma_start(out=x_sb[m][:], in_=x[128 * m : 128 * m + 128, :])
 
-        def load_scales(plane, dram):
+        def load_scales(plane, dram, half):
             for q in range(4):
                 nc.sync.dma_start(
                     out=plane[32 * q : 32 * q + 4, :].bitcast(I32).rearrange("r (g n) -> r g n", g=GY),
-                    in_=dram[:, 4 * q : 4 * q + 4, :].bitcast(I32).rearrange("g r n -> r g n"),
+                    in_=dram[:, 4 * q : 4 * q + 4, 512 * half : 512 * half + 512]
+                    .bitcast(I32)
+                    .rearrange("g r n -> r g n"),
                 )
 
         def load_words(tile, dram, half):
@@ -80,15 +84,22 @@ def tile_hyperalignment_cross_product_s12_kernel(
                 in_=dram[:, :, 1024 * half : 1024 * half + 1024].bitcast(I32).rearrange("g p n -> p g n"),
             )
 
-        nc.vector.memset(ysr[:].bitcast(I32), 0)
-        nc.vector.memset(bs[:].rearrange("p g n -> p (g n)").bitcast(I32), 0)
+        def flat(tile):
+            return tile[:].rearrange("p g n -> p (g n)")
+
+        nc.vector.memset(ysr[0][:].bitcast(I32), 0)
+        nc.vector.memset(flat(bs[0]).bitcast(I32), 0)
         make_identity(nc, ident[:])
         nc.gpsimd.memset(wrow[:], 0.0)
         nc.vector.tensor_copy(
             out=perm[:].rearrange("p (j a i) -> p j a i", j=4, a=4),
             in_=ident[:].rearrange("p (a j i) -> p j a i", a=4, j=4),
         )
+        nc.vector.memset(blank[:], 0.0)
+        nc.vector.quantize_mx(out=blank_codes[:].bitcast(FP8X4), scales=blank_scales[:], in_=blank[:])
         nc.vector.tensor_copy(out=identb[:], in_=ident[:])
+        nc.vector.memset(ysr[1][:].bitcast(I32), 0)
+        nc.vector.memset(flat(bs[1]).bitcast(I32), 0)
 
         rot_v = rot.rearrange("(g p j) d -> g p j d", g=GX, j=4)
         pr_v = prior.rearrange("(c p) e -> p c e", p=128)
@@ -98,27 +109,42 @@ def tile_hyperalignment_cross_product_s12_kernel(
                 nc.sync.dma_start(out=rraw[e][g][:], in_=rot_v[g][:, :, 512 * e : 512 * e + 512])
 
         load_x(0)
-        load_scales(ysr[:], y_scales)
-        for m in range(1, 5):
-            load_x(m)
-        load_scales(bs[:].rearrange("p g n -> p (g n)"), b_scales)
-        load_x(5)
+        load_scales(ysr[0], y_scales, 0)
+        load_x(1)
         load_words(yraw[0][:], y_words, 0)
-        load_words(braw[0][:].rearrange("p g n -> p (g n)"), b_words, 0)
-        load_x(6)
-        load_x(7)
+        load_scales(flat(bs[0]), b_scales, 0)
+        load_words(flat(braw[0]), b_words, 0)
+        for m in range(2, 5):
+            load_x(m)
+        load_scales(ysr[1], y_scales, 1)
+        for m in range(5, 8):
+            load_x(m)
         load_words(yraw[1][:], y_words, 1)
         for h in range(2):
             nc.sync.dma_start(
                 out=wrow[4 * h : 4 * h + 4, :].rearrange("j (q i) -> j q i", i=8),
                 in_=weight.rearrange("(h q j i) -> h j q i", h=2, j=4, i=8)[h],
             )
+        nc.sync.dma_start(out=wrow[8:16, :], in_=gain.rearrange("(r n) -> r n", r=8))
         load_rot(0)
-        nc.sync.dma_start(out=gb[:], in_=gain.partition_broadcast(128))
         load_rot(1)
         nc.sync.dma_start(out=pr[:, 0:4, :], in_=pr_v[:, 0:4, :])
-        load_words(braw[1][:].rearrange("p g n -> p (g n)"), b_words, 1)
+        load_scales(flat(bs[1]), b_scales, 1)
+        load_words(flat(braw[1]), b_words, 1)
         nc.sync.dma_start(out=pr[:, 4:8, :], in_=pr_v[:, 4:8, :])
+
+        def warm(passes):
+            bank = psum.tile([P, 512], F32, name="ev", tag="ev")
+            for k in range(passes):
+                nc.tensor.matmul_mx(
+                    out=bank[:],
+                    lhsT=blank_codes[:, 0:128].bitcast(FP8X4),
+                    lhsT_scale=blank_scales[:, 0:128],
+                    rhs=blank_codes[:].bitcast(FP8X4),
+                    rhs_scale=blank_scales[:],
+                    start=(k == 0),
+                    stop=(k == passes - 1),
+                )
 
         rin = {}
 
@@ -150,46 +176,30 @@ def tile_hyperalignment_cross_product_s12_kernel(
                 in_=yraw[h][:].bitcast(I32).rearrange("p (s j w) -> p j s w", j=4, w=4),
             )
 
-        def permute_ys():
+        def permute_ys(h):
             nc.vector.tensor_copy(
-                out=ysp[:].bitcast(I32).rearrange("p (j s w) -> p j s w", j=4, w=2),
-                in_=ysr[:].bitcast(I32).rearrange("p (s j w) -> p j s w", j=4, w=2),
+                out=ysp[h][:].bitcast(I32).rearrange("p (j s w) -> p j s w", j=4, w=2),
+                in_=ysr[h][:].bitcast(I32).rearrange("p (s j w) -> p j s w", j=4, w=2),
             )
 
-        def template(h, e, n, dst):
-            bank = psum.tile([P, 4, 128], F32, name="ev", tag="ev")
-            for j in range(4):
-                for g in range(GY):
-                    nc.tensor.matmul_mx(
-                        out=bank[:, j, :],
-                        lhsT=yp[h][:, 1024 * j + 256 * g : 1024 * j + 256 * g + 256].bitcast(FP4X4),
-                        lhsT_scale=ysp[:, 1024 * j + 256 * g + 128 * h : 1024 * j + 256 * g + 128 * h + 128],
-                        rhs=braw[e][:, g, 256 * n : 256 * n + 256].bitcast(FP4X4),
-                        rhs_scale=bs[:, g, 512 * e + 128 * n : 512 * e + 128 * n + 128],
-                        start=(g == 0),
-                        stop=(g == GY - 1),
-                    )
-            nc.scalar.copy(out=dst, in_=bank[:].rearrange("p j n -> p n j"))
-
-        def template_wide(h, n2):
-            for jp in range(2):
-                bank = psum.tile([P, 2, 256], F32, name="ev", tag="ev")
-                for k in range(2):
-                    j = 2 * jp + k
+        def template(h, c0, width, dst):
+            e, off = c0 // 512, c0 % 512
+            per = 512 // width
+            for j0 in range(0, 4, per):
+                bank = psum.tile([P, per, width], F32, name="ev", tag="ev")
+                for k in range(per):
                     for g in range(GY):
+                        first = 1024 * (j0 + k) + 256 * g
                         nc.tensor.matmul_mx(
                             out=bank[:, k, :],
-                            lhsT=yp[h][:, 1024 * j + 256 * g : 1024 * j + 256 * g + 256].bitcast(FP4X4),
-                            lhsT_scale=ysp[:, 1024 * j + 256 * g + 128 * h : 1024 * j + 256 * g + 128 * h + 128],
-                            rhs=braw[0][:, g, 512 * n2 : 512 * n2 + 512].bitcast(FP4X4),
-                            rhs_scale=bs[:, g, 256 * n2 : 256 * n2 + 256],
+                            lhsT=yp[h][:, first : first + 256].bitcast(FP4X4),
+                            lhsT_scale=ysp[h][:, first // 2 : first // 2 + 128],
+                            rhs=braw[e][:, g, 2 * off : 2 * (off + width)].bitcast(FP4X4),
+                            rhs_scale=bs[e][:, g, off : off + width],
                             start=(g == 0),
                             stop=(g == GY - 1),
                         )
-                nc.scalar.copy(
-                    out=tin[h][:, 256 * n2 : 256 * n2 + 256, 2 * jp : 2 * jp + 2],
-                    in_=bank[:].rearrange("p j n -> p n j"),
-                )
+                nc.scalar.copy(out=dst[:, :, j0 : j0 + per], in_=bank[:].rearrange("p j n -> p n j"))
 
         def quant(codes, scales, src):
             nc.vector.quantize_mx(out=codes.bitcast(FP8X4), scales=scales, in_=src)
@@ -279,77 +289,85 @@ def tile_hyperalignment_cross_product_s12_kernel(
             eng.tensor_tensor(out=res[:], in0=tmp[:], in1=pr[:, c, 0:512], op=ADD)
             nc.sync.dma_start(out=out[128 * c : 128 * c + 128, 0:512], in_=res[:])
 
-        def template_quant(n, src):
-            quant(
-                ucd[n][:].rearrange("p h n -> p (h n)"),
-                usc[n][:].rearrange("p h n -> p (h n)"),
-                src[:].rearrange("p h n j -> p (h n j)"),
-            )
+        def template_right(h, c0, width):
+            uin[h, c0] = pair.tile([P, width, 4], BF16, name="uin", tag=f"uin{h}", align_bytes=64)
+            template(h, c0, width, uin[h, c0])
 
-        def cross_narrow(n, c0, count):
-            bank = psum.tile([P, 4, 128], F32, name="st", tag="tr")
+        def quant_right(h, c0, width):
+            ucd[h, c0] = kt(f"ucd{h}{c0}", [P, width], U32)
+            usc[h, c0] = kt(f"usc{h}{c0}", [P, width], U8)
+            quant(ucd[h, c0][:], usc[h, c0][:], uin[h, c0][:].rearrange("p n j -> p (n j)"))
+
+        def cross_right(c0, width, d0, count):
+            bank = psum.tile([P, count, width], F32, name="st", tag="tr")
             for k in range(count):
-                c = c0 + k
                 for h in range(2):
                     nc.tensor.matmul_mx(
                         out=bank[:, k, :],
-                        lhsT=acd[c][:, h, :].bitcast(FP8X4),
-                        lhsT_scale=asc[c][:, h, :],
-                        rhs=ucd[n][:, h, :].bitcast(FP8X4),
-                        rhs_scale=usc[n][:, h, :],
+                        lhsT=acd[d0 + k][:, h, :].bitcast(FP8X4),
+                        lhsT_scale=asc[d0 + k][:, h, :],
+                        rhs=ucd[h, c0][:].bitcast(FP8X4),
+                        rhs_scale=usc[h, c0][:],
                         start=(h == 0),
                         stop=(h == 1),
                     )
             return bank
 
-        def gain_narrow(n, count, bank):
-            cols = slice(512 + 128 * n, 512 + 128 * n + 128)
-            tmp = work.tile([P, 4, 128], F32, name="tmp", tag="tmp")
+        def gain_right(c0, width, count, bank):
+            tmp = work.tile([P, count, width], F32, name="tmp", tag="tmp")
             nc.vector.tensor_tensor(
-                out=tmp[:, 0:count, :],
-                in0=bank[:, 0:count, :],
-                in1=gb[:, cols].unsqueeze(1).to_broadcast([P, count, 128]),
+                out=tmp[:],
+                in0=bank[:],
+                in1=gb[:, c0 : c0 + width].unsqueeze(1).to_broadcast([P, count, width]),
                 op=MULT,
             )
             return tmp
 
-        def finish_narrow(n, c0, count, tmp, eng):
-            cols = slice(512 + 128 * n, 512 + 128 * n + 128)
-            res = work.tile([P, 4, 128], F32, name="res", tag="res")
-            eng.tensor_tensor(
-                out=res[:, 0:count, :], in0=tmp[:, 0:count, :], in1=pr[:, c0 : c0 + count, cols], op=ADD
-            )
-            nc.sync.dma_start(
-                out=out.rearrange("(c p) e -> p c e", p=128)[:, c0 : c0 + count, cols], in_=res[:, 0:count, :]
-            )
+        def finish_right(c0, width, d0, count, tmp, eng):
+            cols = slice(c0, c0 + width)
+            res = work.tile([P, count, width], F32, name="res", tag="res")
+            eng.tensor_tensor(out=res[:], in0=tmp[:], in1=pr[:, d0 : d0 + count, cols], op=ADD)
+            nc.sync.dma_start(out=out.rearrange("(c p) e -> p c e", p=128)[:, d0 : d0 + count, cols], in_=res[:])
 
-        xpose([0, 1, 2, 3], "SV")
-        xpose([4, 5], "SVS")
-        permute_ys()
-        quant_x(0, 0)
+        def tslice(h, n):
+            return tin[h][:, 256 * n : 256 * n + 256, :]
+
+        warm(4)
+        xpose([0], "SV")
+        permute_ys(0)
         permute_y(0)
-        template_wide(0, 0)
+        warm(1)
+        xpose([1], "SV")
+        warm(1)
+        template(0, 0, 256, tslice(0, 0))
+        xpose([2, 3, 4], "VS")
+        quant_x(0, 0)
+        template(0, 256, 256, tslice(0, 1))
         quant_x(0, 1)
         quant_x(0, 2)
-        xpose([6, 7], "SVS")
+        permute_ys(1)
         permute_y(1)
+        inter_rot(0, 0, False)
+        xpose([5, 6, 7], "SV")
         wbank = psum.tile([P, P], BF16, name="wbank", tag="tr")
         nc.tensor.transpose(wbank[:], wrow[:], identb[:])
-        nc.vector.tensor_copy(out=wcol[:], in_=wbank[:, 0:8])
-        template_wide(0, 1)
+        nc.vector.tensor_copy(out=wcol[:], in_=wbank[:, 0:16])
         quant_x(1, 0)
-        nc.vector.tensor_copy(out=wcolf[:], in_=wcol[:])
-        quant_x(1, 1)
-        quant_x(1, 2)
-        inter_rot(0, 0, False)
+        nc.vector.tensor_copy(out=wcolf[:], in_=wcol[:, 0:8])
         inter_rot(0, 2, True)
-        inter_rot(0, 1, False)
-        template_wide(1, 0)
+        template(1, 0, 256, tslice(1, 0))
         quant_rot(0, 0)
+        quant_x(1, 1)
+        inter_rot(0, 1, False)
+        quant_x(1, 2)
         quant_rot(0, 1)
         quant_rot(0, 2)
         quant(tcd[0][:], tsc[0][:], tin[0][:].rearrange("p n j -> p (n j)"))
-        template_wide(1, 1)
+        template(1, 256, 256, tslice(1, 1))
+        gbank = psum.tile([P, 8, P], BF16, name="gbank", tag="tr")
+        for r in range(8):
+            nc.tensor.transpose(gbank[:, r, :], wcol[:, 8 + r : 9 + r].to_broadcast([P, P]), identb[:])
+        nc.scalar.copy(out=gb[:].rearrange("p (r n) -> p r n", r=8), in_=gbank[:])
 
         pending = None
         tmp = None
@@ -366,31 +384,33 @@ def tile_hyperalignment_cross_product_s12_kernel(
                 tmp = gain_wide(st)
             aligned_quant(c, ain)
             if pending is not None:
-                finish_wide(pending, tmp, nc.gpsimd if c in (1, 2, 3, 4) else nc.vector)
+                finish_wide(pending, tmp, nc.vector)
             pending = c
             if c in (1, 2):
                 quant_rot(1, c - 1)
             if c < 3:
                 inter_rot(1, c, True)
 
-        uin = {}
-        for n in range(4):
-            uin[n] = pair.tile([P, 2, 128, 4], BF16, name="uin", tag="uin", align_bytes=64)
+        chunks = [(c0, 128) for c0 in range(512, 1024, 128)]
+        for k, (c0, width) in enumerate(chunks):
             for h in range(2):
-                template(h, 1, n, uin[n][:, h, :, :])
-            if n == 0:
+                template_right(h, c0, width)
+            if k == 0:
                 st = cross_wide(7)
                 tmp = gain_wide(st)
-                template_quant(0, uin[0])
+                quant_right(0, c0, width)
+                quant_right(1, c0, width)
                 finish_wide(7, tmp, nc.vector)
                 continue
-            sts = [cross_narrow(n - 1, c0, 4) for c0 in (0, 4)]
-            template_quant(n, uin[n])
-            tmps = [gain_narrow(n - 1, 4, st) for st in sts]
-            for c0, tmp in zip((0, 4), tmps):
-                finish_narrow(n - 1, c0, 4, tmp, nc.gpsimd if n == 3 else nc.vector)
+            last0, lastw = chunks[k - 1]
+            sts = [cross_right(last0, lastw, d0, 4) for d0 in (0, 4)]
+            quant_right(0, c0, width)
+            quant_right(1, c0, width)
+            tmps = [gain_right(last0, lastw, 4, st) for st in sts]
+            for d0, tmp in zip((0, 4), tmps):
+                finish_right(last0, lastw, d0, 4, tmp, nc.vector)
         parts = [(0, 4), (4, 2), (6, 2)]
-        sts = [cross_narrow(3, c0, count) for c0, count in parts]
-        tmps = [gain_narrow(3, count, st) for (c0, count), st in zip(parts, sts)]
-        for (c0, count), tmp in zip(parts, tmps):
-            finish_narrow(3, c0, count, tmp, nc.gpsimd if c0 == 4 else nc.vector)
+        sts = [cross_right(c0, width, d0, count) for d0, count in parts]
+        tmps = [gain_right(c0, width, count, st) for (d0, count), st in zip(parts, sts)]
+        for (d0, count), tmp in zip(parts, tmps):
+            finish_right(c0, width, d0, count, tmp, nc.gpsimd if d0 == 4 else nc.vector)

@@ -57,7 +57,7 @@ def tile_hyperalignment_cross_product_s12_kernel(
         pr = kt("pr", [P, 8, D], BF16)
         gb = kt("gb", [P, D], BF16)
         ident = kt("ident", [P, P], F32)
-        blank = kt("blank", [P, 2048], BF16)
+        blank = stage.tile([P, 2048], BF16, name="blank", tag="rin", align_bytes=64)
         blank_codes = kt("blank_codes", [P, 512], U32)
         blank_scales = kt("blank_scales", [P, 512], U8)
         perm = kt("perm", [P, P], F32)
@@ -113,7 +113,11 @@ def tile_hyperalignment_cross_product_s12_kernel(
         load_x(1)
         load_words(yraw[0][:], y_words, 0)
         load_scales(flat(bs[0]), b_scales, 0)
-        load_words(flat(braw[0]), b_words, 0)
+        for first in (0, 512):
+            nc.sync.dma_start(
+                out=braw[0][:, :, first : first + 512].bitcast(I32),
+                in_=b_words[:, :, first : first + 512].bitcast(I32).rearrange("g p n -> p g n"),
+            )
         for m in range(2, 5):
             load_x(m)
         load_scales(ysr[1], y_scales, 1)
@@ -126,11 +130,11 @@ def tile_hyperalignment_cross_product_s12_kernel(
                 in_=weight.rearrange("(h q j i) -> h j q i", h=2, j=4, i=8)[h],
             )
         nc.sync.dma_start(out=wrow[8:16, :], in_=gain.rearrange("(r n) -> r n", r=8))
+        load_scales(flat(bs[1]), b_scales, 1)
+        load_words(flat(braw[1]), b_words, 1)
         load_rot(0)
         load_rot(1)
         nc.sync.dma_start(out=pr[:, 0:4, :], in_=pr_v[:, 0:4, :])
-        load_scales(flat(bs[1]), b_scales, 1)
-        load_words(flat(braw[1]), b_words, 1)
         nc.sync.dma_start(out=pr[:, 4:8, :], in_=pr_v[:, 4:8, :])
 
         def warm(passes):
@@ -347,70 +351,85 @@ def tile_hyperalignment_cross_product_s12_kernel(
         quant_x(0, 2)
         permute_ys(1)
         permute_y(1)
-        inter_rot(0, 0, False)
-        xpose([5, 6, 7], "SV")
+        xpose([5, 6, 7], "VS")
         wbank = psum.tile([P, P], BF16, name="wbank", tag="tr")
         nc.tensor.transpose(wbank[:], wrow[:], identb[:])
         nc.vector.tensor_copy(out=wcol[:], in_=wbank[:, 0:16])
         quant_x(1, 0)
         nc.vector.tensor_copy(out=wcolf[:], in_=wcol[:, 0:8])
-        inter_rot(0, 2, True)
-        template(1, 0, 256, tslice(1, 0))
-        quant_rot(0, 0)
         quant_x(1, 1)
-        inter_rot(0, 1, False)
         quant_x(1, 2)
-        quant_rot(0, 1)
-        quant_rot(0, 2)
-        quant(tcd[0][:], tsc[0][:], tin[0][:].rearrange("p n j -> p (n j)"))
+        template(1, 0, 256, tslice(1, 0))
+        inter_rot(0, 0, False)
         template(1, 256, 256, tslice(1, 1))
         gbank = psum.tile([P, 8, P], BF16, name="gbank", tag="tr")
         for r in range(8):
             nc.tensor.transpose(gbank[:, r, :], wcol[:, 8 + r : 9 + r].to_broadcast([P, P]), identb[:])
+        quant(tcd[0][:], tsc[0][:], tin[0][:].rearrange("p n j -> p (n j)"))
+        quant_rot(0, 0)
+        inter_rot(0, 1, False)
+        quant_rot(0, 1)
+        inter_rot(0, 2, False)
+        quant_rot(0, 2)
+        quant(tcd[1][:], tsc[1][:], tin[1][:].rearrange("p n j -> p (n j)"))
+        template_right(0, 512, 256)
+        quant_right(0, 512, 256)
+        template_right(1, 512, 256)
         nc.scalar.copy(out=gb[:].rearrange("p (r n) -> p r n", r=8), in_=gbank[:])
+        inter_rot(1, 0, True)
+        inter_rot(1, 1, True)
+        inter_rot(1, 2, True)
 
-        pending = None
-        tmp = None
+        def crosses(c):
+            return cross_wide(c), cross_right(512, 256, c, 1)
+
+        def gains(sts):
+            return gain_wide(sts[0]), gain_right(512, 256, 1, sts[1])
+
+        GPC = (1, 2, 3)
+
+        def finishes(c, tmps, eng):
+            finish_wide(c, tmps[0], eng)
+            finish_right(512, 256, c, 1, tmps[1], eng)
+
         for c in range(8):
             banks = aligned_mm(c)
-            if pending is not None:
-                st = cross_wide(pending)
-            ain = aligned_weigh(banks, c in (4, 5, 6, 7))
+            if c > 0:
+                sts = crosses(c - 1)
+            ain = aligned_weigh(banks, c > 2)
             if c == 0:
-                quant(tcd[1][:], tsc[1][:], tin[1][:].rearrange("p n j -> p (n j)"))
-            if c == 3:
-                quant_rot(1, 2)
-            if pending is not None:
-                tmp = gain_wide(st)
-            aligned_quant(c, ain)
-            if pending is not None:
-                finish_wide(pending, tmp, nc.vector)
-            pending = c
-            if c in (1, 2):
+                quant_right(1, 512, 256)
+            if c in (1, 2, 3):
                 quant_rot(1, c - 1)
-            if c < 3:
-                inter_rot(1, c, True)
+            if c > 0:
+                tmps = gains(sts)
+            aligned_quant(c, ain)
+            if c > 0:
+                finishes(c - 1, tmps, nc.gpsimd if c in GPC else nc.vector)
 
-        chunks = [(c0, 128) for c0 in range(512, 1024, 128)]
-        for k, (c0, width) in enumerate(chunks):
-            for h in range(2):
-                template_right(h, c0, width)
-            if k == 0:
-                st = cross_wide(7)
-                tmp = gain_wide(st)
-                quant_right(0, c0, width)
-                quant_right(1, c0, width)
-                finish_wide(7, tmp, nc.vector)
-                continue
-            last0, lastw = chunks[k - 1]
-            sts = [cross_right(last0, lastw, d0, 4) for d0 in (0, 4)]
-            quant_right(0, c0, width)
-            quant_right(1, c0, width)
-            tmps = [gain_right(last0, lastw, 4, st) for st in sts]
-            for d0, tmp in zip((0, 4), tmps):
-                finish_right(last0, lastw, d0, 4, tmp, nc.vector)
+        def right_piece(c0, d0, count, eng):
+            st = cross_right(c0, 128, d0, count)
+            return lambda: finish_right(c0, 128, d0, count, gain_right(c0, 128, count, st), eng)
+
+        template_right(0, 768, 128)
+        template_right(1, 768, 128)
+        sts = crosses(7)
+        tmps = gains(sts)
+        quant_right(0, 768, 128)
+        quant_right(1, 768, 128)
+        finishes(7, tmps, nc.vector)
+        template_right(0, 896, 128)
+        st = cross_right(768, 128, 0, 4)
+        tmp = gain_right(768, 128, 4, st)
+        quant_right(0, 896, 128)
+        finish_right(768, 128, 0, 4, tmp, nc.vector)
+        template_right(1, 896, 128)
+        st = cross_right(768, 128, 4, 4)
+        quant_right(1, 896, 128)
+        tmp = gain_right(768, 128, 4, st)
+        finish_right(768, 128, 4, 4, tmp, nc.gpsimd)
         parts = [(0, 4), (4, 2), (6, 2)]
-        sts = [cross_right(c0, width, d0, count) for d0, count in parts]
-        tmps = [gain_right(c0, width, count, st) for (d0, count), st in zip(parts, sts)]
+        sts = [cross_right(896, 128, d0, count) for d0, count in parts]
+        tmps = [gain_right(896, 128, count, st) for (d0, count), st in zip(parts, sts)]
         for (d0, count), tmp in zip(parts, tmps):
-            finish_right(c0, width, d0, count, tmp, nc.gpsimd if d0 == 4 else nc.vector)
+            finish_right(896, 128, d0, count, tmp, nc.vector)

from contextlib import ExitStack

import concourse.mybir as mybir
from concourse.masks import make_identity

F32 = mybir.dt.float32
BF16 = mybir.dt.bfloat16
I32 = mybir.dt.int32
U32 = mybir.dt.uint32
U8 = mybir.dt.uint8
FP8X4 = mybir.dt.float8_e4m3fn_x4
FP4X4 = mybir.dt.float4_e2m1fn_x4
MULT = mybir.AluOpType.mult
ADD = mybir.AluOpType.add

T, V, F, D = 1024, 1536, 2048, 1024
P = 128
GX = V // 512
GY = F // 512
FLOPS = 2 * T * D * (V + F) + 2 * D * D * T


def tile_hyperalignment_cross_product_s12_kernel(
    tc, x, rot, weight, y_words, y_scales, b_words, b_scales, gain, prior, out
):
    nc = tc.nc
    with ExitStack() as ctx:
        keep = ctx.enter_context(tc.tile_pool(name="keep", bufs=1))
        stage = ctx.enter_context(tc.tile_pool(name="stage", bufs=4))
        pair = ctx.enter_context(tc.tile_pool(name="pair", bufs=2))
        work = ctx.enter_context(tc.tile_pool(name="work", bufs=5))
        psum = ctx.enter_context(tc.psum_pool(name="psum", bufs=4))
        ctx.enter_context(tc.manual_schedule())

        def kt(name, shape, dtype):
            return keep.tile(shape, dtype, name=name, tag=name, align_bytes=64)

        x_sb = [kt(f"x{m}", [P, V], BF16) for m in range(8)]
        ysr = [kt(f"ysr{h}", [P, GY * 512], U8) for h in range(2)]
        ysp = [kt(f"ysp{h}", [P, GY * 512], U8) for h in range(2)]
        bs = [kt(f"bs{e}", [P, GY, 512], U8) for e in range(2)]
        yraw = [kt(f"yraw{h}", [P, GY * 1024], U8) for h in range(2)]
        yp = [kt(f"yp{h}", [P, GY * 1024], U8) for h in range(2)]
        braw = [kt(f"braw{e}", [P, GY, 1024], U8) for e in range(2)]
        rraw = [[kt(f"rraw{e}{g}", [P, 4, 512], BF16) for g in range(GX)] for e in range(2)]
        rc = [[kt(f"rc{e}{g}", [P, 512], U32) for g in range(GX)] for e in range(2)]
        rs = [[kt(f"rs{e}{g}", [P, 512], U8) for g in range(GX)] for e in range(2)]
        xin = [[kt(f"xin{h}{g}", [P, 2048], BF16) for g in range(GX)] for h in range(2)]
        xc = [[kt(f"xc{h}{g}", [P, 512], U32) for g in range(GX)] for h in range(2)]
        xs = [[kt(f"xs{h}{g}", [P, 512], U8) for g in range(GX)] for h in range(2)]
        tin = [kt(f"tin{h}", [P, 512, 4], BF16) for h in range(2)]
        tcd = [kt(f"tcd{h}", [P, 512], U32) for h in range(2)]
        tsc = [kt(f"tsc{h}", [P, 512], U8) for h in range(2)]
        uin, ucd, usc = {}, {}, {}
        acd = [kt(f"acd{c}", [P, 2, 128], U32) for c in range(8)]
        asc = [kt(f"asc{c}", [P, 2, 128], U8) for c in range(8)]
        pr = kt("pr", [P, 8, D], BF16)
        gb = kt("gb", [P, D], BF16)
        ident = kt("ident", [P, P], F32)
        blank = stage.tile([P, 2048], BF16, name="blank", tag="rin", align_bytes=64)
        blank_codes = kt("blank_codes", [P, 512], U32)
        blank_scales = kt("blank_scales", [P, 512], U8)
        perm = kt("perm", [P, P], F32)
        identb = kt("identb", [P, P], BF16)
        wrow = kt("wrow", [P, P], BF16)
        wcol = kt("wcol", [P, 16], BF16)
        wcolf = kt("wcolf", [P, 8], F32)

        def load_x(m):
            nc.sync.dma_start(out=x_sb[m][:], in_=x[128 * m : 128 * m + 128, :])

        def load_scales(plane, dram, half):
            for q in range(4):
                nc.sync.dma_start(
                    out=plane[32 * q : 32 * q + 4, :].bitcast(I32).rearrange("r (g n) -> r g n", g=GY),
                    in_=dram[:, 4 * q : 4 * q + 4, 512 * half : 512 * half + 512]
                    .bitcast(I32)
                    .rearrange("g r n -> r g n"),
                )

        def load_words(tile, dram, half):
            nc.sync.dma_start(
                out=tile.bitcast(I32).rearrange("p (g n) -> p g n", g=GY),
                in_=dram[:, :, 1024 * half : 1024 * half + 1024].bitcast(I32).rearrange("g p n -> p g n"),
            )

        def flat(tile):
            return tile[:].rearrange("p g n -> p (g n)")

        nc.vector.memset(ysr[0][:].bitcast(I32), 0)
        nc.vector.memset(flat(bs[0]).bitcast(I32), 0)
        make_identity(nc, ident[:])
        nc.gpsimd.memset(wrow[:], 0.0)
        nc.vector.tensor_copy(
            out=perm[:].rearrange("p (j a i) -> p j a i", j=4, a=4),
            in_=ident[:].rearrange("p (a j i) -> p j a i", a=4, j=4),
        )
        nc.vector.memset(blank[:], 0.0)
        nc.vector.quantize_mx(out=blank_codes[:].bitcast(FP8X4), scales=blank_scales[:], in_=blank[:])
        nc.vector.tensor_copy(out=identb[:], in_=ident[:])
        nc.vector.memset(ysr[1][:].bitcast(I32), 0)
        nc.vector.memset(flat(bs[1]).bitcast(I32), 0)

        rot_v = rot.rearrange("(g p j) d -> g p j d", g=GX, j=4)
        pr_v = prior.rearrange("(c p) e -> p c e", p=128)

        def load_rot(e):
            for g in range(GX):
                nc.sync.dma_start(out=rraw[e][g][:], in_=rot_v[g][:, :, 512 * e : 512 * e + 512])

        load_x(0)
        load_scales(ysr[0], y_scales, 0)
        load_x(1)
        load_words(yraw[0][:], y_words, 0)
        load_scales(flat(bs[0]), b_scales, 0)
        for first in (0, 512):
            nc.sync.dma_start(
                out=braw[0][:, :, first : first + 512].bitcast(I32),
                in_=b_words[:, :, first : first + 512].bitcast(I32).rearrange("g p n -> p g n"),
            )
        for m in range(2, 5):
            load_x(m)
        load_scales(ysr[1], y_scales, 1)
        for m in range(5, 8):
            load_x(m)
        load_words(yraw[1][:], y_words, 1)
        for h in range(2):
            nc.sync.dma_start(
                out=wrow[4 * h : 4 * h + 4, :].rearrange("j (q i) -> j q i", i=8),
                in_=weight.rearrange("(h q j i) -> h j q i", h=2, j=4, i=8)[h],
            )
        nc.sync.dma_start(out=wrow[8:16, :], in_=gain.rearrange("(r n) -> r n", r=8))
        load_scales(flat(bs[1]), b_scales, 1)
        load_words(flat(braw[1]), b_words, 1)
        load_rot(0)
        load_rot(1)
        nc.sync.dma_start(out=pr[:, 0:4, :], in_=pr_v[:, 0:4, :])
        nc.sync.dma_start(out=pr[:, 4:8, :], in_=pr_v[:, 4:8, :])

        def warm(passes):
            bank = psum.tile([P, 512], F32, name="ev", tag="ev")
            for k in range(passes):
                nc.tensor.matmul_mx(
                    out=bank[:],
                    lhsT=blank_codes[:, 0:128].bitcast(FP8X4),
                    lhsT_scale=blank_scales[:, 0:128],
                    rhs=blank_codes[:].bitcast(FP8X4),
                    rhs_scale=blank_scales[:],
                    start=(k == 0),
                    stop=(k == passes - 1),
                )

        rin = {}

        def xpose(tiles, engines):
            todo = [(m, g) for m in tiles for g in range(GX)]
            for k in range(0, len(todo), 2):
                two = todo[k : k + 2]
                on_scalar = engines[(k // 2) % len(engines)] == "S"
                bank = psum.tile([P, 2, 2, 128], F32, name="bank", tag="tr")
                for s, (m, g) in enumerate(two):
                    words = x_sb[m][:].bitcast(F32)
                    for u in range(2):
                        nc.tensor.transpose(
                            bank[:, s, u, :], words[:, 256 * g + u : 256 * (g + 1) : 2], perm[:]
                        )
                for s, (m, g) in enumerate(two):
                    h, mm = m // 4, m % 4
                    dst = xin[h][g][:].bitcast(F32).rearrange("p (j c u) -> p j c u", j=4, u=2)
                    dst = dst[:, :, 32 * mm : 32 * mm + 32, :]
                    srcv = bank[:, s, :, :].rearrange("p u (j c) -> p j c u", j=4)
                    if on_scalar:
                        nc.scalar.copy(out=dst, in_=srcv)
                    else:
                        nc.vector.tensor_copy(out=dst, in_=srcv)

        def permute_y(h):
            nc.vector.tensor_copy(
                out=yp[h][:].bitcast(I32).rearrange("p (j s w) -> p j s w", j=4, w=4),
                in_=yraw[h][:].bitcast(I32).rearrange("p (s j w) -> p j s w", j=4, w=4),
            )

        def permute_ys(h):
            nc.vector.tensor_copy(
                out=ysp[h][:].bitcast(I32).rearrange("p (j s w) -> p j s w", j=4, w=2),
                in_=ysr[h][:].bitcast(I32).rearrange("p (s j w) -> p j s w", j=4, w=2),
            )

        def template(h, c0, width, dst):
            e, off = c0 // 512, c0 % 512
            per = 512 // width
            for j0 in range(0, 4, per):
                bank = psum.tile([P, per, width], F32, name="ev", tag="ev")
                for k in range(per):
                    for g in range(GY):
                        first = 1024 * (j0 + k) + 256 * g
                        nc.tensor.matmul_mx(
                            out=bank[:, k, :],
                            lhsT=yp[h][:, first : first + 256].bitcast(FP4X4),
                            lhsT_scale=ysp[h][:, first // 2 : first // 2 + 128],
                            rhs=braw[e][:, g, 2 * off : 2 * (off + width)].bitcast(FP4X4),
                            rhs_scale=bs[e][:, g, off : off + width],
                            start=(g == 0),
                            stop=(g == GY - 1),
                        )
                nc.scalar.copy(out=dst[:, :, j0 : j0 + per], in_=bank[:].rearrange("p j n -> p n j"))

        def quant(codes, scales, src):
            nc.vector.quantize_mx(out=codes.bitcast(FP8X4), scales=scales, in_=src)

        def quant_x(h, g):
            quant(xc[h][g][:], xs[h][g][:], xin[h][g][:])

        def inter_rot(e, g, on_scalar):
            rin[e, g] = stage.tile([P, 2048], BF16, name="rin", tag="rin", align_bytes=64)
            dst = rin[e, g][:].rearrange("p (c i t) -> p c t i", i=4, t=4)
            srcv = rraw[e][g][:].rearrange("p t (c i) -> p c t i", i=4)
            if on_scalar:
                nc.scalar.copy(out=dst, in_=srcv)
            else:
                nc.vector.tensor_copy(out=dst, in_=srcv)

        def quant_rot(e, g):
            quant(rc[e][g][:], rs[e][g][:], rin[e, g][:])

        def aligned_mm(c):
            e, cc = c // 4, c % 4
            banks = []
            for h in range(2):
                bank = psum.tile([P, 4, 128], F32, name="ev", tag="ev")
                for j in range(4):
                    for g in range(GX):
                        nc.tensor.matmul_mx(
                            out=bank[:, j, :],
                            lhsT=xc[h][g][:, 128 * j : 128 * j + 128].bitcast(FP8X4),
                            lhsT_scale=xs[h][g][:, 128 * j : 128 * j + 128],
                            rhs=rc[e][g][:, 128 * cc : 128 * cc + 128].bitcast(FP8X4),
                            rhs_scale=rs[e][g][:, 128 * cc : 128 * cc + 128],
                            start=(g == 0),
                            stop=(g == GX - 1),
                        )
                banks.append(bank)
            return banks

        def aligned_weigh(banks, share):
            ain = pair.tile([P, 2, 128, 4], BF16, name="ain", tag="ain", align_bytes=64)
            for h in range(2):
                if h == 0 and share:
                    for j in range(4):
                        nc.scalar.activation(
                            out=ain[:, h, :, j],
                            in_=banks[h][:, j, :],
                            func=mybir.ActivationFunctionType.Copy,
                            scale=wcolf[:, 4 * h + j : 4 * h + j + 1],
                        )
                    continue
                nc.vector.tensor_tensor(
                    out=ain[:, h, :, :],
                    in0=banks[h][:].rearrange("p j n -> p n j"),
                    in1=wcol[:, 4 * h : 4 * h + 4].unsqueeze(1).to_broadcast([P, 128, 4]),
                    op=MULT,
                )
            return ain

        def aligned_quant(c, ain):
            quant(
                acd[c][:].rearrange("p h n -> p (h n)"),
                asc[c][:].rearrange("p h n -> p (h n)"),
                ain[:].rearrange("p h n j -> p (h n j)"),
            )

        def cross_wide(c):
            bank = psum.tile([P, 512], F32, name="st", tag="tr")
            for h in range(2):
                nc.tensor.matmul_mx(
                    out=bank[:],
                    lhsT=acd[c][:, h, :].bitcast(FP8X4),
                    lhsT_scale=asc[c][:, h, :],
                    rhs=tcd[h][:].bitcast(FP8X4),
                    rhs_scale=tsc[h][:],
                    start=(h == 0),
                    stop=(h == 1),
                )
            return bank

        def gain_wide(bank):
            tmp = work.tile([P, 512], F32, name="tmp", tag="tmp")
            nc.vector.tensor_tensor(out=tmp[:], in0=bank[:], in1=gb[:, 0:512], op=MULT)
            return tmp

        def finish_wide(c, tmp, eng):
            res = work.tile([P, 512], F32, name="res", tag="res")
            eng.tensor_tensor(out=res[:], in0=tmp[:], in1=pr[:, c, 0:512], op=ADD)
            nc.sync.dma_start(out=out[128 * c : 128 * c + 128, 0:512], in_=res[:])

        def template_right(h, c0, width):
            uin[h, c0] = pair.tile([P, width, 4], BF16, name="uin", tag=f"uin{h}", align_bytes=64)
            template(h, c0, width, uin[h, c0])

        def quant_right(h, c0, width):
            ucd[h, c0] = kt(f"ucd{h}{c0}", [P, width], U32)
            usc[h, c0] = kt(f"usc{h}{c0}", [P, width], U8)
            quant(ucd[h, c0][:], usc[h, c0][:], uin[h, c0][:].rearrange("p n j -> p (n j)"))

        def cross_right(c0, width, d0, count):
            bank = psum.tile([P, count, width], F32, name="st", tag="tr")
            for k in range(count):
                for h in range(2):
                    nc.tensor.matmul_mx(
                        out=bank[:, k, :],
                        lhsT=acd[d0 + k][:, h, :].bitcast(FP8X4),
                        lhsT_scale=asc[d0 + k][:, h, :],
                        rhs=ucd[h, c0][:].bitcast(FP8X4),
                        rhs_scale=usc[h, c0][:],
                        start=(h == 0),
                        stop=(h == 1),
                    )
            return bank

        def gain_right(c0, width, count, bank):
            tmp = work.tile([P, count, width], F32, name="tmp", tag="tmp")
            nc.vector.tensor_tensor(
                out=tmp[:],
                in0=bank[:],
                in1=gb[:, c0 : c0 + width].unsqueeze(1).to_broadcast([P, count, width]),
                op=MULT,
            )
            return tmp

        def finish_right(c0, width, d0, count, tmp, eng):
            cols = slice(c0, c0 + width)
            res = work.tile([P, count, width], F32, name="res", tag="res")
            eng.tensor_tensor(out=res[:], in0=tmp[:], in1=pr[:, d0 : d0 + count, cols], op=ADD)
            nc.sync.dma_start(out=out.rearrange("(c p) e -> p c e", p=128)[:, d0 : d0 + count, cols], in_=res[:])

        def tslice(h, n):
            return tin[h][:, 256 * n : 256 * n + 256, :]

        warm(4)
        xpose([0], "SV")
        permute_ys(0)
        permute_y(0)
        warm(1)
        xpose([1], "SV")
        warm(1)
        template(0, 0, 256, tslice(0, 0))
        xpose([2, 3, 4], "VS")
        quant_x(0, 0)
        template(0, 256, 256, tslice(0, 1))
        quant_x(0, 1)
        quant_x(0, 2)
        permute_ys(1)
        permute_y(1)
        xpose([5, 6, 7], "VS")
        wbank = psum.tile([P, P], BF16, name="wbank", tag="tr")
        nc.tensor.transpose(wbank[:], wrow[:], identb[:])
        nc.vector.tensor_copy(out=wcol[:], in_=wbank[:, 0:16])
        quant_x(1, 0)
        nc.vector.tensor_copy(out=wcolf[:], in_=wcol[:, 0:8])
        quant_x(1, 1)
        quant_x(1, 2)
        template(1, 0, 256, tslice(1, 0))
        inter_rot(0, 0, False)
        template(1, 256, 256, tslice(1, 1))
        gbank = psum.tile([P, 8, P], BF16, name="gbank", tag="tr")
        for r in range(8):
            nc.tensor.transpose(gbank[:, r, :], wcol[:, 8 + r : 9 + r].to_broadcast([P, P]), identb[:])
        quant(tcd[0][:], tsc[0][:], tin[0][:].rearrange("p n j -> p (n j)"))
        quant_rot(0, 0)
        inter_rot(0, 1, False)
        quant_rot(0, 1)
        inter_rot(0, 2, False)
        quant_rot(0, 2)
        quant(tcd[1][:], tsc[1][:], tin[1][:].rearrange("p n j -> p (n j)"))
        template_right(0, 512, 256)
        quant_right(0, 512, 256)
        template_right(1, 512, 256)
        nc.scalar.copy(out=gb[:].rearrange("p (r n) -> p r n", r=8), in_=gbank[:])
        inter_rot(1, 0, True)
        inter_rot(1, 1, True)
        inter_rot(1, 2, True)

        def crosses(c):
            return cross_wide(c), cross_right(512, 256, c, 1)

        def gains(sts):
            return gain_wide(sts[0]), gain_right(512, 256, 1, sts[1])

        GPC = (1, 2, 3)

        def finishes(c, tmps, eng):
            finish_wide(c, tmps[0], eng)
            finish_right(512, 256, c, 1, tmps[1], eng)

        for c in range(8):
            banks = aligned_mm(c)
            if c > 0:
                sts = crosses(c - 1)
            ain = aligned_weigh(banks, c > 2)
            if c == 0:
                quant_right(1, 512, 256)
            if c in (1, 2, 3):
                quant_rot(1, c - 1)
            if c > 0:
                tmps = gains(sts)
            aligned_quant(c, ain)
            if c > 0:
                finishes(c - 1, tmps, nc.gpsimd if c in GPC else nc.vector)

        def right_piece(c0, d0, count, eng):
            st = cross_right(c0, 128, d0, count)
            return lambda: finish_right(c0, 128, d0, count, gain_right(c0, 128, count, st), eng)

        template_right(0, 768, 128)
        template_right(1, 768, 128)
        sts = crosses(7)
        tmps = gains(sts)
        quant_right(0, 768, 128)
        quant_right(1, 768, 128)
        finishes(7, tmps, nc.vector)
        template_right(0, 896, 128)
        st = cross_right(768, 128, 0, 4)
        tmp = gain_right(768, 128, 4, st)
        quant_right(0, 896, 128)
        finish_right(768, 128, 0, 4, tmp, nc.vector)
        template_right(1, 896, 128)
        st = cross_right(768, 128, 4, 4)
        quant_right(1, 896, 128)
        tmp = gain_right(768, 128, 4, st)
        finish_right(768, 128, 4, 4, tmp, nc.gpsimd)
        parts = [(0, 4), (4, 2), (6, 2)]
        sts = [cross_right(896, 128, d0, count) for d0, count in parts]
        tmps = [gain_right(896, 128, count, st) for (d0, count), st in zip(parts, sts)]
        for (d0, count), tmp in zip(parts, tmps):
            finish_right(896, 128, d0, count, tmp, nc.vector)
